import numpy as np
import ml_dtypes


def mxq(x, axis, fmt="e4m3"):
    dtype, down = {"e4m3": (ml_dtypes.float8_e4m3fn, 7), "e5m2": (ml_dtypes.float8_e5m2, 14)}[fmt]
    v = np.moveaxis(np.asarray(x, np.float32).astype(ml_dtypes.bfloat16).astype(np.float64), axis, -1)
    blocks = v.reshape(v.shape[:-1] + (-1, 32))
    amax = np.abs(blocks).max(-1, keepdims=True)
    byte = np.maximum(np.where(amax > 0, np.frexp(amax)[1] - 1 + 127, 0) - down, 1)
    scale = np.exp2(byte - 127.0)
    codes = (blocks / scale).astype(np.float32).astype(dtype).astype(np.float64)
    return np.moveaxis((codes * scale).reshape(v.shape), -1, axis)


WIDE = False


def mx_kscale(k):
    if not WIDE:
        return np.ones(k)
    levels = np.array([10, -10, 5, -5, 0])
    if k % 512:
        return np.exp2(np.random.permutation(np.resize(levels, k // 32))).repeat(32)
    a = np.empty((k // 512, 16))
    for p in range(k // 512):
        a[p, :8] = np.random.permutation(np.resize(levels, 8))
        for g in range(8):
            far = levels[np.abs(levels - a[p, g]) >= 10]
            a[p, g + 8] = far[np.random.randint(len(far))]
    return np.exp2(a.ravel()).repeat(32)


def f64(x):
    return np.asarray(x).astype(np.float64)


def striped(idx):
    return np.tile(idx.reshape(-1, 16).T, (8, 1)).astype(np.uint16)


def unstriped(offs):
    return offs[:16].T.reshape(-1).astype(np.int64)


def pack_weight(w):
    k, n = w.shape
    w = f64(np.asarray(w, np.float32).astype(ml_dtypes.bfloat16)).reshape(k // 32, 32, n)
    amax = np.abs(w).max(1)
    byte = np.clip(np.where(amax > 0, np.frexp(amax)[1] - 1 + 127 - 7, 1), 1, 254)
    scaled = (w * np.exp2(127.0 - byte)[:, None, :]).reshape(k, n).astype(np.float32)
    words = np.ascontiguousarray(scaled.reshape(k // 512, 128, 4, n).transpose(0, 1, 3, 2)).astype(ml_dtypes.float8_e4m3fn).view(np.uint8)
    return words, np.ascontiguousarray(byte.astype(np.uint8).reshape(k // 512, 16, n))


def unpack_weight(words, scales):
    g, p, n, _ = words.shape
    vals = np.ascontiguousarray(words).view(ml_dtypes.float8_e4m3fn).astype(np.float64) * np.repeat(np.exp2(scales.astype(np.float64) - 127.0), 8, axis=1)[..., None]
    return vals.transpose(0, 1, 3, 2).reshape(g * 512, n)


def sigmoid(v):
    return 1.0 / (1.0 + np.exp(-np.maximum(v, -700.0)))


K, T, S, N = 512, 1024, 512, 256


def setup_inputs():
    n = np.random.standard_normal
    s = mx_kscale(K)[:, None]
    packed_xT = pack_weight(n((K, T)) * s)
    return {
        "x_words": packed_xT[0],
        "x_scales": packed_xT[1],
        "w1": (n((K, N)) / np.sqrt(K) / s).astype(np.float32),
        "w2": (n((K, N)) / np.sqrt(K) / s).astype(np.float32),
        "pred": (n((N, S))).astype(np.float32),
        "offs": striped(np.random.permutation(T)[:S]),
    }


def reference(x_words, x_scales, w1, w2, pred, offs):
    xq = unpack_weight(x_words, x_scales)[:, unstriped(offs)]
    yf = mxq(f64(w1), 0, "e4m3").T @ xq
    yg = mxq(f64(w2), 0, "e4m3").T @ xq
    gain = 0.9 * sigmoid(yg)
    base0 = yf - (gain * (np.pad(f64(pred), ((0, 0), (0, 1)))[:, 1:]))
    base1 = base0 + gain * (np.pad(base0, ((0, 0), (0, 1)))[:, 1:])
    gg1 = gain * (np.pad(gain, ((0, 0), (0, 1)))[:, 1:])
    base2 = base1 + gg1 * (np.pad(base1, ((0, 0), (0, 2)))[:, 2:])
    gg2 = gg1 * (np.pad(gg1, ((0, 0), (0, 2)))[:, 2:])
    return base2 + gg2 * (np.pad(yf, ((0, 0), (0, 4)))[:, 4:])

@@ -1,0 +1,176 @@
+from contextlib import ExitStack
+
+import concourse.mybir as mybir
+from concourse.masks import make_identity
+
+K, T, S, N = 512, 1024, 512, 256
+FLOPS = 2 * 2 * K * S * N
+
+F32 = mybir.dt.float32
+BF16 = mybir.dt.bfloat16
+I32 = mybir.dt.int32
+U32 = mybir.dt.uint32
+U16 = mybir.dt.uint16
+U8 = mybir.dt.uint8
+FP8X4 = mybir.dt.float8_e4m3fn_x4
+ALU = mybir.AluOpType
+ACT = mybir.ActivationFunctionType
+
+P = 128
+HALF = 256
+ROW = S + 8
+GAIN = 0.9
+
+
+def tile_picked_yrts_mean_p_kernel(tc, x_words, x_scales, w1, w2, pred, offs, out):
+    nc = tc.nc
+    with ExitStack() as ctx:
+        keep = ctx.enter_context(tc.tile_pool(name="keep", bufs=1))
+        psum = ctx.enter_context(tc.psum_pool(name="psum", bufs=1))
+
+        offsets = keep.tile([P, S // 16], U16, name="offsets")
+        nc.sync.dma_start(offsets[:], offs)
+
+        xs_rows = keep.tile([P, T // 4], I32, name="xs_rows", align_bytes=64)
+        for q in range(4):
+            nc.sync.dma_start(out=xs_rows[32 * q : 32 * q + 4, :], in_=x_scales[0, 4 * q : 4 * q + 4, :].bitcast(I32))
+        xs_all = keep.tile([P, T], U8, name="xs_all", align_bytes=64)
+        nc.gpsimd.memset(xs_all[:].bitcast(I32), 0)
+
+        def load_w(w, b, name):
+            raw = keep.tile([P, 4, P], F32, name=name)
+            nc.sync.dma_start(out=raw[:], in_=w[:, b * P : (b + 1) * P].rearrange("(p j) c -> p j c", j=4))
+            return raw
+
+        def load_pred(b, lo, hi, name):
+            t = keep.tile([P, hi - lo], F32, name=name)
+            nc.sync.dma_start(out=t[:], in_=pred[b * P : (b + 1) * P, lo:hi])
+            return t
+
+        w2_raw0 = load_w(w2, 0, "w2_raw0")
+        xw_all = keep.tile([P, T], I32, name="xw_all", align_bytes=64)
+        nc.sync.dma_start(out=xw_all[:], in_=x_words[0].rearrange("p n t -> p (n t)").bitcast(I32))
+        w1_raw0 = load_w(w1, 0, "w1_raw0")
+        pred0 = load_pred(0, 0, S, "pred0")
+        w2_raw1 = load_w(w2, 1, "w2_raw1")
+        w1_raw1 = load_w(w1, 1, "w1_raw1")
+        pred1 = load_pred(1, 0, S, "pred1")
+        preds = [pred0, pred1]
+
+        ident = keep.tile([P, P], F32, name="ident")
+        make_identity(nc, ident[:])
+        rows = keep.tile([P, 8 * ROW], F32, name="rows")
+        nc.gpsimd.memset(rows[:].rearrange("p (r c) -> p r c", c=ROW)[:, :, S:ROW], 0.0)
+
+        warm = keep.tile([P, 1], F32, name="warm")
+        nc.scalar.activation(warm[:], rows[:, S : S + 1], ACT.Sigmoid)
+
+        def quant(raw, name, eng):
+            grouped = keep.tile([P, P, 4], BF16, name=name + "_bf", align_bytes=64)
+            if eng == "s":
+                nc.scalar.copy(out=grouped[:], in_=raw[:].rearrange("p j c -> p c j"))
+            elif eng == "g":
+                nc.gpsimd.tensor_scalar(out=grouped[:], in0=raw[:].rearrange("p j c -> p c j"), scalar1=1.0, scalar2=0.0, op0=ALU.mult, op1=ALU.add)
+            else:
+                nc.vector.tensor_copy(out=grouped[:], in_=raw[:].rearrange("p j c -> p c j"))
+            codes = keep.tile([P, P], U32, name=name + "_codes", align_bytes=64)
+            scales = keep.tile([P, P], U8, name=name + "_scales", align_bytes=64)
+            nc.vector.quantize_mx(out=codes[:].bitcast(FP8X4), scales=scales[:], in_=grouped[:].rearrange("p c j -> p (c j)"))
+            return codes, scales
+
+        for q in range(4):
+            nc.vector.tensor_copy(xs_all[32 * q : 32 * q + 4, :].bitcast(I32), xs_rows[32 * q : 32 * q + 4, :])
+        xs = keep.tile([P, S], U8, name="xs", align_bytes=64)
+        nc.vector.tensor_copy(xs[:], xs_all[:].indirect(offsets[:]))
+        w2q0 = quant(w2_raw0, "w2q0", "s")
+        xw = {}
+        for h in (1, 0):
+            xw[h] = keep.tile([P, HALF], U32, name="xw%d" % h, align_bytes=64)
+            nc.vector.tensor_copy(xw[h][:], xw_all[:].bitcast(U32).indirect(offsets[:, h * 16 : (h + 1) * 16]))
+        w1q0 = quant(w1_raw0, "w1q0", "v")
+
+        def gate(b, h, w2q):
+            ygt = psum.tile([P, 2, P], F32, name="ygt%d%d" % (b, h), tag="ygt%d" % h)
+            for t in range(2):
+                nc.tensor.matmul_mx(out=ygt[:, t, :], lhsT=xw[h][:, t * P : (t + 1) * P].bitcast(FP8X4),
+                                    lhsT_scale=xs[:, h * HALF + t * P : h * HALF + (t + 1) * P],
+                                    rhs=w2q[0][:].bitcast(FP8X4), rhs_scale=w2q[1][:], start=True, stop=True)
+            sgt = keep.tile([P, 2, P], F32, name="sgt%d%d" % (b, h))
+            nc.scalar.activation(sgt[:], ygt[:], ACT.Sigmoid)
+            return sgt
+
+        def turn(sgt, sg):
+            for t in range(2):
+                nc.tensor.transpose(sg[:, t * P : (t + 1) * P], sgt[:, t, :], ident[:])
+
+        def mean(h, w1q, yf):
+            nc.tensor.matmul_mx(out=yf, lhsT=w1q[0][:].bitcast(FP8X4), lhsT_scale=w1q[1][:],
+                                rhs=xw[h][:].bitcast(FP8X4), rhs_scale=xs[:, h * HALF : (h + 1) * HALF], start=True, stop=True)
+
+        sg = {}
+        yf = {}
+        for h in (1, 0):
+            sgt = gate(0, h, w2q0)
+            yft = psum.tile([P, HALF], F32, name="yf0%d" % h)
+            mean(h, w1q0, yft[:])
+            yf[0, h] = yft[:]
+            sgp = psum.tile([P, HALF], F32, name="sg0%d" % h)
+            turn(sgt, sgp[:])
+            sg[0, h] = sgp[:]
+
+        w2q1 = quant(w2_raw1, "w2q1", "s")
+        w1q1 = quant(w1_raw1, "w1q1", "s")
+        yf1 = psum.tile([P, S], F32, name="yf1")
+        sg1 = psum.tile([P, S], F32, name="sg1")
+        sgts = {}
+        for h in (1, 0):
+            sgts[h] = gate(1, h, w2q1)
+        for h in (1, 0):
+            yf[1, h] = yf1[:, h * HALF : (h + 1) * HALF]
+            mean(h, w1q1, yf[1, h])
+        for h in (1, 0):
+            sg[1, h] = sg1[:, h * HALF : (h + 1) * HALF]
+            turn(sgts[h], sg[1, h])
+
+        def row(b, r, lo, shift):
+            base = (4 * b + r) * ROW + lo + shift
+            return rows[:, base : base + HALF]
+
+        def smooth(b, h, last):
+            lo = h * HALF
+            add = nc.vector if last else nc.gpsimd
+            s, f = sg[b, h], yf[b, h]
+
+            def gained(dst, src):
+                nc.vector.scalar_tensor_tensor(out=dst, in0=s, scalar=GAIN, in1=src, op0=ALU.mult, op1=ALU.mult)
+
+            def innovation():
+                if b >= 0:
+                    nc.vector.tensor_tensor(row(b, 0, lo, 0), f, preds[b][:, lo : lo + HALF], ALU.subtract)
+                else:
+                    fs = keep.tile([P, HALF], F32, name="fs_%d" % h)
+                    nc.scalar.copy(out=fs[:], in_=f)
+                    nc.gpsimd.tensor_tensor(row(b, 0, lo, 0), fs[:], preds[b][:, lo : lo + HALF], ALU.subtract)
+
+            e2 = keep.tile([P, HALF], F32, name="e2_%d%d" % (b, h))
+            v = keep.tile([P, HALF], F32, name="v_%d%d" % (b, h))
+            x = keep.tile([P, HALF], F32, name="x_%d%d" % (b, h))
+            res = keep.tile([P, HALF], F32, name="res_%d%d" % (b, h))
+            return [
+                innovation,
+                lambda: gained(row(b, 1, lo, 0), row(b, 0, lo, 1)),
+                lambda: gained(e2[:], row(b, 1, lo, 1)),
+                lambda: add.tensor_tensor(row(b, 2, lo, 0), row(b, 1, lo, 0), e2[:], ALU.add),
+                lambda: gained(row(b, 3, lo, 0), row(b, 2, lo, 1)),
+                lambda: nc.vector.tensor_tensor(x[:], f, row(b, 2, lo, 0), ALU.add),
+                lambda: gained(v[:], row(b, 3, lo, 1)),
+                lambda: add.tensor_tensor(res[:], x[:], v[:], ALU.add),
+                lambda: nc.sync.dma_start(out=out[b * P : (b + 1) * P, lo : lo + HALF], in_=res[:]),
+            ]
+
+        chains = [smooth(0, 1, False), smooth(0, 0, False), smooth(1, 1, False), smooth(1, 0, True)]
+        for steps in (range(0, 4), range(4, 9)):
+            for pair in (chains[:2], chains[2:]):
+                for i in steps:
+                    for c in pair:
+                        c[i]()

@@ -48,7 +48,7 @@ def tile_picked_yrts_mean_p_kernel(tc, x_words, x_scales, w1, w2, pred, offs, ou
             return t
 
         w2_raw0 = load_w(w2, 0, "w2_raw0")
-        xw_all = keep.tile([P, T], I32, name="xw_all", align_bytes=64)
+        xw_all = keep.tile([P, T], I32, name="xw_all", tag="xw_all", align_bytes=64)
         nc.sync.dma_start(out=xw_all[:], in_=x_words[0].rearrange("p n t -> p (n t)").bitcast(I32))
         w1_raw0 = load_w(w1, 0, "w1_raw0")
         pred0 = load_pred(0, 0, S, "pred0")
@@ -65,15 +65,15 @@ def tile_picked_yrts_mean_p_kernel(tc, x_words, x_scales, w1, w2, pred, offs, ou
         warm = keep.tile([P, 1], F32, name="warm")
         nc.scalar.activation(warm[:], rows[:, S : S + 1], ACT.Sigmoid)
 
-        def quant(raw, name, eng):
-            grouped = keep.tile([P, P, 4], BF16, name=name + "_bf", align_bytes=64)
+        def quant(raw, name, eng, bf_tag, codes_tag):
+            grouped = keep.tile([P, P, 4], BF16, name=name + "_bf", tag=bf_tag, align_bytes=64)
             if eng == "s":
                 nc.scalar.copy(out=grouped[:], in_=raw[:].rearrange("p j c -> p c j"))
             elif eng == "g":
                 nc.gpsimd.tensor_scalar(out=grouped[:], in0=raw[:].rearrange("p j c -> p c j"), scalar1=1.0, scalar2=0.0, op0=ALU.mult, op1=ALU.add)
             else:
                 nc.vector.tensor_copy(out=grouped[:], in_=raw[:].rearrange("p j c -> p c j"))
-            codes = keep.tile([P, P], U32, name=name + "_codes", align_bytes=64)
+            codes = keep.tile([P, P], U32, name=name + "_codes", tag=codes_tag, align_bytes=64)
             scales = keep.tile([P, P], U8, name=name + "_scales", align_bytes=64)
             nc.vector.quantize_mx(out=codes[:].bitcast(FP8X4), scales=scales[:], in_=grouped[:].rearrange("p c j -> p (c j)"))
             return codes, scales
@@ -82,12 +82,15 @@ def tile_picked_yrts_mean_p_kernel(tc, x_words, x_scales, w1, w2, pred, offs, ou
             nc.vector.tensor_copy(xs_all[32 * q : 32 * q + 4, :].bitcast(I32), xs_rows[32 * q : 32 * q + 4, :])
         xs = keep.tile([P, S], U8, name="xs", align_bytes=64)
         nc.vector.tensor_copy(xs[:], xs_all[:].indirect(offsets[:]))
-        w2q0 = quant(w2_raw0, "w2q0", "s")
+        w2q0 = quant(w2_raw0, "w2q0", "s", "w2q0_bf", "w2q0_codes")
         xw = {}
-        for h in (1, 0):
-            xw[h] = keep.tile([P, HALF], U32, name="xw%d" % h, align_bytes=64)
+        def gather(h, tag):
+            xw[h] = keep.tile([P, HALF], U32, name="xw%d" % h, tag=tag, align_bytes=64)
             nc.vector.tensor_copy(xw[h][:], xw_all[:].bitcast(U32).indirect(offsets[:, h * 16 : (h + 1) * 16]))
-        w1q0 = quant(w1_raw0, "w1q0", "v")
+
+        gather(1, "xw1")
+        gather(0, "w2q0_bf")
+        w1q0 = quant(w1_raw0, "w1q0", "s", "w1q0_bf", "xw_all")
 
         def gate(b, h, w2q):
             ygt = psum.tile([P, 2, P], F32, name="ygt%d%d" % (b, h), tag="ygt%d" % h)
@@ -118,8 +121,8 @@ def tile_picked_yrts_mean_p_kernel(tc, x_words, x_scales, w1, w2, pred, offs, ou
             turn(sgt, sgp[:])
             sg[0, h] = sgp[:]
 
-        w2q1 = quant(w2_raw1, "w2q1", "s")
-        w1q1 = quant(w1_raw1, "w1q1", "s")
+        w2q1 = quant(w2_raw1, "w2q1", "s", "w2q0_codes", "w2q1_codes")
+        w1q1 = quant(w1_raw1, "w1q1", "s", "xw_all", "w1q1_codes")
         yf1 = psum.tile([P, S], F32, name="yf1")
         sg1 = psum.tile([P, S], F32, name="sg1")
         sgts = {}
@@ -160,7 +163,7 @@ def tile_picked_yrts_mean_p_kernel(tc, x_words, x_scales, w1, w2, pred, offs, ou
                 innovation,
                 lambda: gained(row(b, 1, lo, 0), row(b, 0, lo, 1)),
                 lambda: gained(e2[:], row(b, 1, lo, 1)),
-                lambda: add.tensor_tensor(row(b, 2, lo, 0), row(b, 1, lo, 0), e2[:], ALU.add),
+                lambda: nc.gpsimd.tensor_tensor(row(b, 2, lo, 0), row(b, 1, lo, 0), e2[:], ALU.add),
                 lambda: gained(row(b, 3, lo, 0), row(b, 2, lo, 1)),
                 lambda: nc.vector.tensor_tensor(x[:], f, row(b, 2, lo, 0), ALU.add),
                 lambda: gained(v[:], row(b, 3, lo, 1)),

from contextlib import ExitStack

import concourse.mybir as mybir
from concourse.masks import make_identity

K, T, S, N = 512, 1024, 512, 256
FLOPS = 2 * 2 * K * S * N

F32 = mybir.dt.float32
BF16 = mybir.dt.bfloat16
I32 = mybir.dt.int32
U32 = mybir.dt.uint32
U16 = mybir.dt.uint16
U8 = mybir.dt.uint8
FP8X4 = mybir.dt.float8_e4m3fn_x4
ALU = mybir.AluOpType
ACT = mybir.ActivationFunctionType

P = 128
HALF = 256
ROW = S + 8
GAIN = 0.9


def tile_picked_yrts_mean_p_kernel(tc, x_words, x_scales, w1, w2, pred, offs, out):
    nc = tc.nc
    with ExitStack() as ctx:
        keep = ctx.enter_context(tc.tile_pool(name="keep", bufs=1))
        psum = ctx.enter_context(tc.psum_pool(name="psum", bufs=1))

        offsets = keep.tile([P, S // 16], U16, name="offsets")
        nc.sync.dma_start(offsets[:], offs)

        xs_rows = keep.tile([P, T // 4], I32, name="xs_rows", align_bytes=64)
        for q in range(4):
            nc.sync.dma_start(out=xs_rows[32 * q : 32 * q + 4, :], in_=x_scales[0, 4 * q : 4 * q + 4, :].bitcast(I32))
        xs_all = keep.tile([P, T], U8, name="xs_all", align_bytes=64)
        nc.gpsimd.memset(xs_all[:].bitcast(I32), 0)

        def load_w(w, b, name):
            raw = keep.tile([P, 4, P], F32, name=name)
            nc.sync.dma_start(out=raw[:], in_=w[:, b * P : (b + 1) * P].rearrange("(p j) c -> p j c", j=4))
            return raw

        def load_pred(b, lo, hi, name):
            t = keep.tile([P, hi - lo], F32, name=name)
            nc.sync.dma_start(out=t[:], in_=pred[b * P : (b + 1) * P, lo:hi])
            return t

        w2_raw0 = load_w(w2, 0, "w2_raw0")
        xw_all = keep.tile([P, T], I32, name="xw_all", tag="xw_all", align_bytes=64)
        nc.sync.dma_start(out=xw_all[:], in_=x_words[0].rearrange("p n t -> p (n t)").bitcast(I32))
        w1_raw0 = load_w(w1, 0, "w1_raw0")
        pred0 = load_pred(0, 0, S, "pred0")
        w2_raw1 = load_w(w2, 1, "w2_raw1")
        w1_raw1 = load_w(w1, 1, "w1_raw1")
        pred1 = load_pred(1, 0, S, "pred1")
        preds = [pred0, pred1]

        ident = keep.tile([P, P], F32, name="ident")
        make_identity(nc, ident[:])
        rows = keep.tile([P, 8 * ROW], F32, name="rows")
        nc.gpsimd.memset(rows[:].rearrange("p (r c) -> p r c", c=ROW)[:, :, S:ROW], 0.0)

        warm = keep.tile([P, 1], F32, name="warm")
        nc.scalar.activation(warm[:], rows[:, S : S + 1], ACT.Sigmoid)

        def quant(raw, name, eng, bf_tag, codes_tag):
            grouped = keep.tile([P, P, 4], BF16, name=name + "_bf", tag=bf_tag, align_bytes=64)
            if eng == "s":
                nc.scalar.copy(out=grouped[:], in_=raw[:].rearrange("p j c -> p c j"))
            elif eng == "g":
                nc.gpsimd.tensor_scalar(out=grouped[:], in0=raw[:].rearrange("p j c -> p c j"), scalar1=1.0, scalar2=0.0, op0=ALU.mult, op1=ALU.add)
            else:
                nc.vector.tensor_copy(out=grouped[:], in_=raw[:].rearrange("p j c -> p c j"))
            codes = keep.tile([P, P], U32, name=name + "_codes", tag=codes_tag, align_bytes=64)
            scales = keep.tile([P, P], U8, name=name + "_scales", align_bytes=64)
            nc.vector.quantize_mx(out=codes[:].bitcast(FP8X4), scales=scales[:], in_=grouped[:].rearrange("p c j -> p (c j)"))
            return codes, scales

        for q in range(4):
            nc.vector.tensor_copy(xs_all[32 * q : 32 * q + 4, :].bitcast(I32), xs_rows[32 * q : 32 * q + 4, :])
        xs = keep.tile([P, S], U8, name="xs", align_bytes=64)
        nc.vector.tensor_copy(xs[:], xs_all[:].indirect(offsets[:]))
        w2q0 = quant(w2_raw0, "w2q0", "s", "w2q0_bf", "w2q0_codes")
        xw = {}
        def gather(h, tag):
            xw[h] = keep.tile([P, HALF], U32, name="xw%d" % h, tag=tag, align_bytes=64)
            nc.vector.tensor_copy(xw[h][:], xw_all[:].bitcast(U32).indirect(offsets[:, h * 16 : (h + 1) * 16]))

        gather(1, "xw1")
        gather(0, "w2q0_bf")
        w1q0 = quant(w1_raw0, "w1q0", "s", "w1q0_bf", "xw_all")

        def gate(b, h, w2q):
            ygt = psum.tile([P, 2, P], F32, name="ygt%d%d" % (b, h), tag="ygt%d" % h)
            for t in range(2):
                nc.tensor.matmul_mx(out=ygt[:, t, :], lhsT=xw[h][:, t * P : (t + 1) * P].bitcast(FP8X4),
                                    lhsT_scale=xs[:, h * HALF + t * P : h * HALF + (t + 1) * P],
                                    rhs=w2q[0][:].bitcast(FP8X4), rhs_scale=w2q[1][:], start=True, stop=True)
            sgt = keep.tile([P, 2, P], F32, name="sgt%d%d" % (b, h))
            nc.scalar.activation(sgt[:], ygt[:], ACT.Sigmoid)
            return sgt

        def turn(sgt, sg):
            for t in range(2):
                nc.tensor.transpose(sg[:, t * P : (t + 1) * P], sgt[:, t, :], ident[:])

        def mean(h, w1q, yf):
            nc.tensor.matmul_mx(out=yf, lhsT=w1q[0][:].bitcast(FP8X4), lhsT_scale=w1q[1][:],
                                rhs=xw[h][:].bitcast(FP8X4), rhs_scale=xs[:, h * HALF : (h + 1) * HALF], start=True, stop=True)

        sg = {}
        yf = {}
        for h in (1, 0):
            sgt = gate(0, h, w2q0)
            yft = psum.tile([P, HALF], F32, name="yf0%d" % h)
            mean(h, w1q0, yft[:])
            yf[0, h] = yft[:]
            sgp = psum.tile([P, HALF], F32, name="sg0%d" % h)
            turn(sgt, sgp[:])
            sg[0, h] = sgp[:]

        w2q1 = quant(w2_raw1, "w2q1", "s", "w2q0_codes", "w2q1_codes")
        w1q1 = quant(w1_raw1, "w1q1", "s", "xw_all", "w1q1_codes")
        yf1 = psum.tile([P, S], F32, name="yf1")
        sg1 = psum.tile([P, S], F32, name="sg1")
        sgts = {}
        for h in (1, 0):
            sgts[h] = gate(1, h, w2q1)
        for h in (1, 0):
            yf[1, h] = yf1[:, h * HALF : (h + 1) * HALF]
            mean(h, w1q1, yf[1, h])
        for h in (1, 0):
            sg[1, h] = sg1[:, h * HALF : (h + 1) * HALF]
            turn(sgts[h], sg[1, h])

        def row(b, r, lo, shift):
            base = (4 * b + r) * ROW + lo + shift
            return rows[:, base : base + HALF]

        def smooth(b, h, last):
            lo = h * HALF
            add = nc.vector if last else nc.gpsimd
            s, f = sg[b, h], yf[b, h]

            def gained(dst, src):
                nc.vector.scalar_tensor_tensor(out=dst, in0=s, scalar=GAIN, in1=src, op0=ALU.mult, op1=ALU.mult)

            def innovation():
                if b >= 0:
                    nc.vector.tensor_tensor(row(b, 0, lo, 0), f, preds[b][:, lo : lo + HALF], ALU.subtract)
                else:
                    fs = keep.tile([P, HALF], F32, name="fs_%d" % h)
                    nc.scalar.copy(out=fs[:], in_=f)
                    nc.gpsimd.tensor_tensor(row(b, 0, lo, 0), fs[:], preds[b][:, lo : lo + HALF], ALU.subtract)

            e2 = keep.tile([P, HALF], F32, name="e2_%d%d" % (b, h))
            v = keep.tile([P, HALF], F32, name="v_%d%d" % (b, h))
            x = keep.tile([P, HALF], F32, name="x_%d%d" % (b, h))
            res = keep.tile([P, HALF], F32, name="res_%d%d" % (b, h))
            return [
                innovation,
                lambda: gained(row(b, 1, lo, 0), row(b, 0, lo, 1)),
                lambda: gained(e2[:], row(b, 1, lo, 1)),
                lambda: nc.gpsimd.tensor_tensor(row(b, 2, lo, 0), row(b, 1, lo, 0), e2[:], ALU.add),
                lambda: gained(row(b, 3, lo, 0), row(b, 2, lo, 1)),
                lambda: nc.vector.tensor_tensor(x[:], f, row(b, 2, lo, 0), ALU.add),
                lambda: gained(v[:], row(b, 3, lo, 1)),
                lambda: add.tensor_tensor(res[:], x[:], v[:], ALU.add),
                lambda: nc.sync.dma_start(out=out[b * P : (b + 1) * P, lo : lo + HALF], in_=res[:]),
            ]

        chains = [smooth(0, 1, False), smooth(0, 0, False), smooth(1, 1, False), smooth(1, 0, True)]
        for steps in (range(0, 4), range(4, 9)):
            for pair in (chains[:2], chains[2:]):
                for i in steps:
                    for c in pair:
                        c[i]()
